import numpy as np
CORES = [0,7,8,15,16,23,24,31,32,39,40,47,48,55,56,63]
N = 16
def setup_inputs(rng):
    return {"x": rng.standard_normal((N, 128, 256), dtype=np.float32)}
def reference(x):
    s = x.sum(axis=0, dtype=np.float64).astype(x.dtype)
    b = 256 // N
    return {"y": np.stack([s[:, r * b:(r + 1) * b] for r in range(N)])}

@@ -1,0 +1,93 @@
+from concourse.bass import DstId, RemoteDMATransfer
+
+NB = 16
+SCRATCH = {
+    "xb": ("dram", [NB, 128, 16], "float32"),
+    "pa": ("dram", [NB, 128, 16], "float32"),
+    "pb": ("dram", [NB, 128, 16], "float32"),
+    "m": ("dram", [NB, 128, 16], "float32"),
+    "sw": ("dram", [4, 128, 16], "float32"),
+    "fin": ("dram", [128, 16], "float32"),
+}
+SEMAPHORES = ["loaded", "s1", "s2", "s3", "s4", "sent", "stored"]
+
+
+def handler(chip, b):
+    if b // 2 == chip:
+        return 1 - (b & 1)
+    return b & 1
+
+
+def rank_program(g, core, T, topo):
+    k, c = divmod(core, 8)
+    if c not in (0, 3, 7):
+        return
+    A, H, B = 8 * k, 8 * k + 3, 8 * k + 7
+    mate = k ^ 1
+    sem = T.sem
+    sent = [0]
+
+    def did(dst):
+        rid, pid, _se = topo.addr(dst)
+        return DstId(rid=rid, pnc=pid)
+
+    def fused(items, eng, rsem):
+        trs = []
+        for i, (dst, out, srcs) in enumerate(items):
+            mask = ((1 << eng) - 1) << (i * eng)
+            if len(srcs) == 1:
+                trs.append(RemoteDMATransfer(dst_ids=[did(dst)], dma_engine_mask=mask, remote_sem=rsem,
+                                             srcs=srcs, dsts=[out], alu_op=0))
+            else:
+                trs.append(RemoteDMATransfer(dst_ids=[did(dst)], dma_engine_mask=mask, remote_sem=rsem,
+                                             srcs=srcs, dsts=[out], alu_op=1))
+            sent[0] += eng
+        g.remote_dma_fused(trs, local_sem=sem.sent)
+
+    own = [b for b in range(NB) if ((b // 2) & 1) == (k & 1)]
+    oth = [b for b in range(NB) if ((b // 2) & 1) != (k & 1)]
+    ship_H = [b for b in oth if handler(mate, b) == 0]
+    ship_B = [b for b in oth if handler(mate, b) == 1]
+
+    if c == 3:
+        g.wait_ge(sem.s1, 32)
+        fused([(8 * mate, T.m[b], [T.pa[b], T.pb[b]]) for b in ship_H], 2, sem.s2)
+        g.wait_ge(sem.sent, sent[0])
+        return
+
+    me = 0 if c == 0 else 1
+    peer = B if me == 0 else A
+    mine_land = T.pb if me == 0 else T.pa
+    peer_land = T.pa if me == 0 else T.pb
+    hand_me = [b for b in own if handler(k, b) == me]
+    hand_peer = [b for b in own if handler(k, b) != me]
+
+    for b in range(NB):
+        q = g.sync if b % 2 == 0 else g.scalar
+        q.dma_start(T.xb[b], T.x[:, 16 * b:16 * b + 16]).then_inc(sem.loaded, 16)
+    g.wait_ge(sem.loaded, 16 * NB)
+
+    if me == 0:
+        fused([(peer, peer_land[b], [T.xb[b]]) for b in hand_peer + ship_B], 2, sem.s1)
+    else:
+        fused([(peer, peer_land[b], [T.xb[b]]) for b in hand_peer], 4, sem.s1)
+    fused([(H, peer_land[b], [T.xb[b]]) for b in ship_H], 4, sem.s1)
+    g.wait_ge(sem.s1, 16)
+
+    if me == 1:
+        fused([(8 * mate + 7, T.m[b], [T.xb[b], mine_land[b]]) for b in ship_B], 2, sem.s2)
+    g.wait_ge(sem.s2, 8)
+
+    far = [b for b in hand_me if b // 2 != k]
+    fused([(8 * (b // 2) + (7 if handler(b // 2, b) else 0), T.sw[k // 2],
+            [T.xb[b], mine_land[b], T.m[b]]) for b in far], 2, sem.s3)
+    g.wait_ge(sem.s3, 6)
+
+    b = [b for b in hand_me if b // 2 == k][0]
+    srcs = [T.xb[b], mine_land[b], T.m[b]] + [T.sw[j] for j in range(4) if j != k // 2]
+    fused([(peer, T.fin[:, :], srcs)], 16, sem.s4)
+    g.wait_ge(sem.s4, 16)
+    g.sync.wait_ge(sem.s4, 16)
+    g.sync.dma_start(T.y[:, :], T.fin[:, :]).then_inc(sem.stored, 16)
+    g.wait_ge(sem.stored, 16)
+    g.wait_ge(sem.sent, sent[0])

@@ -1,93 +1,129 @@
 from concourse.bass import DstId, RemoteDMATransfer
 
-NB = 16
 SCRATCH = {
-    "xb": ("dram", [NB, 128, 16], "float32"),
-    "pa": ("dram", [NB, 128, 16], "float32"),
-    "pb": ("dram", [NB, 128, 16], "float32"),
-    "m": ("dram", [NB, 128, 16], "float32"),
-    "sw": ("dram", [4, 128, 16], "float32"),
-    "fin": ("dram", [128, 16], "float32"),
+    "xb": ("dram", [16, 128, 16], "float32"),
+    "pa": ("dram", [16, 128, 16], "float32"),
+    "pb": ("dram", [16, 128, 16], "float32"),
+    "m": ("dram", [16, 128, 16], "float32"),
+    "sw": ("dram", [8, 128, 16], "float32"),
+    "fin": ("dram", [2, 128, 16], "float32"),
 }
-SEMAPHORES = ["loaded", "s1", "s2", "s3", "s4", "sent", "stored"]
+STAGE_SEM = {"rawO": "s1o", "rawE": "s1e", "ship": "s2", "switch": "s3", "final": "s4"}
+SEMAPHORES = ["ldO", "ldE", "s1o", "s1e", "s2", "s3", "s4", "sent", "stored"]
+FINISHER = (1, 4)
 
 
-def handler(chip, b):
-    if b // 2 == chip:
-        return 1 - (b & 1)
-    return b & 1
+def worker(k, c, h):
+    if c == k:
+        return FINISHER[h]
+    if (c ^ k) & 1:
+        d = ((c - (k ^ 1)) % 8) // 2
+        if h == 0:
+            return 3 if d == 0 else 2
+        return 7 if d < 2 else 6
+    d = ((c - k) % 8) // 2
+    if h == 0:
+        return 0 if d < 3 else 3
+    return 7 if d == 1 else 5
+
+
+def chip_calls(k):
+    calls = {}
+    for c in range(8):
+        for h in range(2):
+            q, w = 2 * c + h, worker(k, c, h)
+            other_plane = (c ^ k) & 1
+            srcs = []
+            for r, land in ((0, "pa"), (7, "pb")):
+                if w == r:
+                    srcs.append(("xb", q))
+                else:
+                    calls.setdefault((8 * k + r, "rawO" if other_plane else "rawE"), []).append(
+                        ([8 * k + w], (land, q), [("xb", q)]))
+                    srcs.append((land, q))
+            if other_plane:
+                mate = k ^ 1
+                item, stage = ([8 * mate + worker(mate, c, h)], ("m", q), srcs), "ship"
+            elif c != k:
+                item, stage = ([8 * c + FINISHER[h]], ("sw", 2 * (k // 2) + h), srcs + [("m", q)]), "switch"
+            else:
+                srcs = srcs + [("m", q)] + [("sw", 2 * j + h) for j in range(4) if j != k // 2]
+                item, stage = ([8 * k, 8 * k + 7], ("fin", h), srcs), "final"
+            calls.setdefault((8 * k + w, stage), []).append(item)
+    return calls
+
+
+def engines(stage, items):
+    avail = 8 if stage in ("ship", "switch") else 16
+    e = 1
+    while 2 * e * len(items) <= avail:
+        e *= 2
+    return e
 
 
 def rank_program(g, core, T, topo):
-    k, c = divmod(core, 8)
-    if c not in (0, 3, 7):
-        return
-    A, H, B = 8 * k, 8 * k + 3, 8 * k + 7
-    mate = k ^ 1
+    k = core // 8
     sem = T.sem
+    mine = {}
+    expect = {}
+    for kk in range(8):
+        for (src, stage), items in chip_calls(kk).items():
+            if src == core:
+                mine[stage] = items
+            for dsts, _out, _srcs in items:
+                if core in dsts:
+                    s = STAGE_SEM[stage]
+                    expect[s] = expect.get(s, 0) + engines(stage, items)
+    if not mine and not expect:
+        return
     sent = [0]
+    waited = []
 
-    def did(dst):
-        rid, pid, _se = topo.addr(dst)
-        return DstId(rid=rid, pnc=pid)
+    def wait(names):
+        for s in names:
+            if s in expect and s not in waited:
+                g.wait_ge(sem[s], expect[s])
+                waited.append(s)
 
-    def fused(items, eng, rsem):
+    def issue(stage):
+        items = mine[stage]
+        e = engines(stage, items)
         trs = []
-        for i, (dst, out, srcs) in enumerate(items):
-            mask = ((1 << eng) - 1) << (i * eng)
-            if len(srcs) == 1:
-                trs.append(RemoteDMATransfer(dst_ids=[did(dst)], dma_engine_mask=mask, remote_sem=rsem,
-                                             srcs=srcs, dsts=[out], alu_op=0))
-            else:
-                trs.append(RemoteDMATransfer(dst_ids=[did(dst)], dma_engine_mask=mask, remote_sem=rsem,
-                                             srcs=srcs, dsts=[out], alu_op=1))
-            sent[0] += eng
+        for i, (dsts, (ob, oslot), srcs) in enumerate(items):
+            ids = []
+            for d in dsts:
+                rid, pid, _se = topo.addr(d)
+                ids.append(DstId(rid=rid, pnc=pid))
+            trs.append(RemoteDMATransfer(
+                dst_ids=ids, dma_engine_mask=((1 << e) - 1) << (i * e), remote_sem=sem[STAGE_SEM[stage]],
+                srcs=[T[b][s] for b, s in srcs], dsts=[T[ob][oslot] for _d in dsts],
+                alu_op=1 if len(srcs) > 1 else 0))
+            sent[0] += e
         g.remote_dma_fused(trs, local_sem=sem.sent)
 
-    own = [b for b in range(NB) if ((b // 2) & 1) == (k & 1)]
-    oth = [b for b in range(NB) if ((b // 2) & 1) != (k & 1)]
-    ship_H = [b for b in oth if handler(mate, b) == 0]
-    ship_B = [b for b in oth if handler(mate, b) == 1]
-
-    if c == 3:
-        g.wait_ge(sem.s1, 32)
-        fused([(8 * mate, T.m[b], [T.pa[b], T.pb[b]]) for b in ship_H], 2, sem.s2)
-        g.wait_ge(sem.sent, sent[0])
-        return
-
-    me = 0 if c == 0 else 1
-    peer = B if me == 0 else A
-    mine_land = T.pb if me == 0 else T.pa
-    peer_land = T.pa if me == 0 else T.pb
-    hand_me = [b for b in own if handler(k, b) == me]
-    hand_peer = [b for b in own if handler(k, b) != me]
-
-    for b in range(NB):
-        q = g.sync if b % 2 == 0 else g.scalar
-        q.dma_start(T.xb[b], T.x[:, 16 * b:16 * b + 16]).then_inc(sem.loaded, 16)
-    g.wait_ge(sem.loaded, 16 * NB)
-
-    if me == 0:
-        fused([(peer, peer_land[b], [T.xb[b]]) for b in hand_peer + ship_B], 2, sem.s1)
-    else:
-        fused([(peer, peer_land[b], [T.xb[b]]) for b in hand_peer], 4, sem.s1)
-    fused([(H, peer_land[b], [T.xb[b]]) for b in ship_H], 4, sem.s1)
-    g.wait_ge(sem.s1, 16)
-
-    if me == 1:
-        fused([(8 * mate + 7, T.m[b], [T.xb[b], mine_land[b]]) for b in ship_B], 2, sem.s2)
-    g.wait_ge(sem.s2, 8)
-
-    far = [b for b in hand_me if b // 2 != k]
-    fused([(8 * (b // 2) + (7 if handler(b // 2, b) else 0), T.sw[k // 2],
-            [T.xb[b], mine_land[b], T.m[b]]) for b in far], 2, sem.s3)
-    g.wait_ge(sem.s3, 6)
-
-    b = [b for b in hand_me if b // 2 == k][0]
-    srcs = [T.xb[b], mine_land[b], T.m[b]] + [T.sw[j] for j in range(4) if j != k // 2]
-    fused([(peer, T.fin[:, :], srcs)], 16, sem.s4)
-    g.wait_ge(sem.s4, 16)
-    g.sync.wait_ge(sem.s4, 16)
-    g.sync.dma_start(T.y[:, :], T.fin[:, :]).then_inc(sem.stored, 16)
-    g.wait_ge(sem.stored, 16)
+    is_rank = T.rank_of(core) is not None
+    if is_rank:
+        order = [c for c in range(8) if (c ^ k) & 1] + [c for c in range(8) if not (c ^ k) & 1]
+        for i, c in enumerate(order):
+            q = g.sync if i % 2 == 0 else g.scalar
+            q.dma_start(T.xb[2 * c:2 * c + 2], T.x[:, 32 * c:32 * c + 32]).then_inc(sem.ldO if i < 4 else sem.ldE, 16)
+        g.wait_ge(sem.ldO, 64)
+        issue("rawO")
+        g.wait_ge(sem.ldE, 64)
+        issue("rawE")
+    if "ship" in mine:
+        wait(["s1o"])
+        issue("ship")
+    if "switch" in mine:
+        wait(["s1e", "s2"])
+        issue("switch")
+    if "final" in mine:
+        wait(["s1e", "s2", "s3"])
+        issue("final")
+    if is_rank:
+        wait(["s4"])
+        g.sync.wait_ge(sem.s4, expect["s4"])
+        first = 0 if core % 8 == 0 else 1
+        g.sync.dma_start(T.y[:, :], T.fin[:, first:128:2, :]).then_inc(sem.stored, 16)
+        g.wait_ge(sem.stored, 16)
     g.wait_ge(sem.sent, sent[0])

@@ -74,8 +74,6 @@ def rank_program(g, core, T, topo):
                 if core in dsts:
                     s = STAGE_SEM[stage]
                     expect[s] = expect.get(s, 0) + engines(stage, items)
-    if not mine and not expect:
-        return
     sent = [0]
     waited = []
 
@@ -121,9 +119,8 @@ def rank_program(g, core, T, topo):
         wait(["s1e", "s2", "s3"])
         issue("final")
     if is_rank:
-        wait(["s4"])
-        g.sync.wait_ge(sem.s4, expect["s4"])
         first = 0 if core % 8 == 0 else 1
+        g.sync.wait_ge(sem.s4, expect["s4"])
         g.sync.dma_start(T.y[:, :], T.fin[:, first:128:2, :]).then_inc(sem.stored, 16)
         g.wait_ge(sem.stored, 16)
     g.wait_ge(sem.sent, sent[0])

from concourse.bass import DstId, RemoteDMATransfer

SCRATCH = {
    "xb": ("dram", [16, 128, 16], "float32"),
    "pa": ("dram", [16, 128, 16], "float32"),
    "pb": ("dram", [16, 128, 16], "float32"),
    "m": ("dram", [16, 128, 16], "float32"),
    "sw": ("dram", [8, 128, 16], "float32"),
    "fin": ("dram", [2, 128, 16], "float32"),
}
STAGE_SEM = {"rawO": "s1o", "rawE": "s1e", "ship": "s2", "switch": "s3", "final": "s4"}
SEMAPHORES = ["ldO", "ldE", "s1o", "s1e", "s2", "s3", "s4", "sent", "stored"]
FINISHER = (1, 4)


def worker(k, c, h):
    if c == k:
        return FINISHER[h]
    if (c ^ k) & 1:
        d = ((c - (k ^ 1)) % 8) // 2
        if h == 0:
            return 3 if d == 0 else 2
        return 7 if d < 2 else 6
    d = ((c - k) % 8) // 2
    if h == 0:
        return 0 if d < 3 else 3
    return 7 if d == 1 else 5


def chip_calls(k):
    calls = {}
    for c in range(8):
        for h in range(2):
            q, w = 2 * c + h, worker(k, c, h)
            other_plane = (c ^ k) & 1
            srcs = []
            for r, land in ((0, "pa"), (7, "pb")):
                if w == r:
                    srcs.append(("xb", q))
                else:
                    calls.setdefault((8 * k + r, "rawO" if other_plane else "rawE"), []).append(
                        ([8 * k + w], (land, q), [("xb", q)]))
                    srcs.append((land, q))
            if other_plane:
                mate = k ^ 1
                item, stage = ([8 * mate + worker(mate, c, h)], ("m", q), srcs), "ship"
            elif c != k:
                item, stage = ([8 * c + FINISHER[h]], ("sw", 2 * (k // 2) + h), srcs + [("m", q)]), "switch"
            else:
                srcs = srcs + [("m", q)] + [("sw", 2 * j + h) for j in range(4) if j != k // 2]
                item, stage = ([8 * k, 8 * k + 7], ("fin", h), srcs), "final"
            calls.setdefault((8 * k + w, stage), []).append(item)
    return calls


def engines(stage, items):
    avail = 8 if stage in ("ship", "switch") else 16
    e = 1
    while 2 * e * len(items) <= avail:
        e *= 2
    return e


def rank_program(g, core, T, topo):
    k = core // 8
    sem = T.sem
    mine = {}
    expect = {}
    for kk in range(8):
        for (src, stage), items in chip_calls(kk).items():
            if src == core:
                mine[stage] = items
            for dsts, _out, _srcs in items:
                if core in dsts:
                    s = STAGE_SEM[stage]
                    expect[s] = expect.get(s, 0) + engines(stage, items)
    sent = [0]
    waited = []

    def wait(names):
        for s in names:
            if s in expect and s not in waited:
                g.wait_ge(sem[s], expect[s])
                waited.append(s)

    def issue(stage):
        items = mine[stage]
        e = engines(stage, items)
        trs = []
        for i, (dsts, (ob, oslot), srcs) in enumerate(items):
            ids = []
            for d in dsts:
                rid, pid, _se = topo.addr(d)
                ids.append(DstId(rid=rid, pnc=pid))
            trs.append(RemoteDMATransfer(
                dst_ids=ids, dma_engine_mask=((1 << e) - 1) << (i * e), remote_sem=sem[STAGE_SEM[stage]],
                srcs=[T[b][s] for b, s in srcs], dsts=[T[ob][oslot] for _d in dsts],
                alu_op=1 if len(srcs) > 1 else 0))
            sent[0] += e
        g.remote_dma_fused(trs, local_sem=sem.sent)

    is_rank = T.rank_of(core) is not None
    if is_rank:
        order = [c for c in range(8) if (c ^ k) & 1] + [c for c in range(8) if not (c ^ k) & 1]
        for i, c in enumerate(order):
            q = g.sync if i % 2 == 0 else g.scalar
            q.dma_start(T.xb[2 * c:2 * c + 2], T.x[:, 32 * c:32 * c + 32]).then_inc(sem.ldO if i < 4 else sem.ldE, 16)
        g.wait_ge(sem.ldO, 64)
        issue("rawO")
        g.wait_ge(sem.ldE, 64)
        issue("rawE")
    if "ship" in mine:
        wait(["s1o"])
        issue("ship")
    if "switch" in mine:
        wait(["s1e", "s2"])
        issue("switch")
    if "final" in mine:
        wait(["s1e", "s2", "s3"])
        issue("final")
    if is_rank:
        first = 0 if core % 8 == 0 else 1
        g.sync.wait_ge(sem.s4, expect["s4"])
        g.sync.dma_start(T.y[:, :], T.fin[:, first:128:2, :]).then_inc(sem.stored, 16)
        g.wait_ge(sem.stored, 16)
    g.wait_ge(sem.sent, sent[0])
